import numpy as np
import ml_dtypes


def mxq(x, axis, fmt="e4m3"):
    dtype, down = {"e4m3": (ml_dtypes.float8_e4m3fn, 7), "e5m2": (ml_dtypes.float8_e5m2, 14)}[fmt]
    v = np.moveaxis(np.asarray(x, np.float32).astype(ml_dtypes.bfloat16).astype(np.float64), axis, -1)
    blocks = v.reshape(v.shape[:-1] + (-1, 32))
    amax = np.abs(blocks).max(-1, keepdims=True)
    byte = np.maximum(np.where(amax > 0, np.frexp(amax)[1] - 1 + 127, 0) - down, 1)
    scale = np.exp2(byte - 127.0)
    codes = (blocks / scale).astype(np.float32).astype(dtype).astype(np.float64)
    return np.moveaxis((codes * scale).reshape(v.shape), -1, axis)


WIDE = False


def mx_kscale(k):
    if not WIDE:
        return np.ones(k)
    levels = np.array([10, -10, 5, -5, 0])
    if k % 512:
        return np.exp2(np.random.permutation(np.resize(levels, k // 32))).repeat(32)
    a = np.empty((k // 512, 16))
    for p in range(k // 512):
        a[p, :8] = np.random.permutation(np.resize(levels, 8))
        for g in range(8):
            far = levels[np.abs(levels - a[p, g]) >= 10]
            a[p, g + 8] = far[np.random.randint(len(far))]
    return np.exp2(a.ravel()).repeat(32)


def f64(x):
    return np.asarray(x).astype(np.float64)


def striped(idx):
    return np.tile(idx.reshape(-1, 16).T, (8, 1)).astype(np.uint16)


def unstriped(offs):
    return offs[:16].T.reshape(-1).astype(np.int64)


def pack_weight(w):
    k, n = w.shape
    w = f64(np.asarray(w, np.float32).astype(ml_dtypes.bfloat16)).reshape(k // 32, 32, n)
    amax = np.abs(w).max(1)
    byte = np.clip(np.where(amax > 0, np.frexp(amax)[1] - 1 + 127 - 7, 1), 1, 254)
    scaled = (w * np.exp2(127.0 - byte)[:, None, :]).reshape(k, n).astype(np.float32)
    words = np.ascontiguousarray(scaled.reshape(k // 512, 128, 4, n).transpose(0, 1, 3, 2)).astype(ml_dtypes.float8_e4m3fn).view(np.uint8)
    return words, np.ascontiguousarray(byte.astype(np.uint8).reshape(k // 512, 16, n))


def unpack_weight(words, scales):
    g, p, n, _ = words.shape
    vals = np.ascontiguousarray(words).view(ml_dtypes.float8_e4m3fn).astype(np.float64) * np.repeat(np.exp2(scales.astype(np.float64) - 127.0), 8, axis=1)[..., None]
    return vals.transpose(0, 1, 3, 2).reshape(g * 512, n)


def sigmoid(v):
    return 1.0 / (1.0 + np.exp(-np.maximum(v, -700.0)))


K, T, S, D, G, J = 512, 2048, 1024, 8, 128, 512


def setup_inputs():
    n = np.random.standard_normal
    s = mx_kscale(K)[:, None]
    packed_xT = pack_weight(n((K, T)) * s)
    return {
        "x_words": packed_xT[0],
        "x_scales": packed_xT[1],
        "hT": (n((K, J)) / np.sqrt(K) / s).astype(np.float32),
        "offs": striped(np.random.permutation(T)[:S]),
    }


def reference(x_words, x_scales, hT, offs):
    hTq = mxq(f64(hT), 0, "e4m3")
    xq = unpack_weight(x_words, x_scales)[:, unstriped(offs)]
    y = hTq.T @ xq
    return sigmoid(y.reshape(J, G, D).max(axis=2))

@@ -1,0 +1,109 @@
+from contextlib import ExitStack
+
+import concourse.mybir as mybir
+
+K, T, S, D, G, J = 512, 2048, 1024, 8, 128, 512
+FLOPS = 2 * K * J * S
+
+F32 = mybir.dt.float32
+BF16 = mybir.dt.bfloat16
+I32 = mybir.dt.int32
+U32 = mybir.dt.uint32
+U16 = mybir.dt.uint16
+U8 = mybir.dt.uint8
+FP8X4 = mybir.dt.float8_e4m3fn_x4
+SIGMOID = mybir.ActivationFunctionType.Sigmoid
+MAX = mybir.AluOpType.max
+AXIS_X = mybir.AxisListType.X
+
+P = 128
+PACK = 4
+N = 512
+HALF = 256
+
+
+def tile_picked_zlate_sig_p_kernel(tc, x_words, x_scales, hT, offs, out):
+    nc = tc.nc
+    with ExitStack() as ctx:
+        keep = ctx.enter_context(tc.tile_pool(name="keep", bufs=1))
+        psum = ctx.enter_context(tc.psum_pool(name="psum", bufs=1))
+
+        offsets = keep.tile([P, S // 16], U16, name="offsets")
+        nc.sync.dma_start(offsets[:], offs)
+
+        scale_table = keep.tile([P, T], U8, name="scale_table", align_bytes=64)
+        nc.vector.memset(scale_table[:].bitcast(I32), 0)
+        for q in range(4):
+            nc.scalar.dma_start(scale_table[32 * q : 32 * q + 4, :].bitcast(I32), x_scales[0, 4 * q : 4 * q + 4, :].bitcast(I32))
+
+        warm_in = keep.tile([P, 1], F32, name="warm_in")
+        warm_out = keep.tile([P, 1], F32, name="warm_out")
+        nc.vector.memset(warm_in[:], 0.0)
+        nc.scalar.activation(warm_out[:], warm_in[:], SIGMOID)
+
+        h_rows = hT.rearrange("(p j) c -> p j c", j=PACK)
+        h_raw = [keep.tile([P, PACK, HALF], F32, name="h_raw%d" % u) for u in range(2)]
+        word_table = keep.tile([P, T], I32, name="word_table", align_bytes=64)
+        nc.sync.dma_start(h_raw[0][:], h_rows[:, :, 0:HALF])
+        nc.sync.dma_start(word_table[:], x_words[0].rearrange("p n r -> p (n r)").bitcast(I32))
+        nc.sync.dma_start(h_raw[1][:], h_rows[:, :, HALF : 2 * HALF])
+
+        x_scale = keep.tile([P, S], U8, name="x_scale", align_bytes=64)
+        nc.vector.tensor_copy(x_scale[:], scale_table[:].indirect(offsets[:]))
+
+        h_code = []
+        h_scale = []
+
+        def quantize_half(u):
+            grouped = keep.tile([P, HALF, PACK], BF16, name="grouped%d" % u, align_bytes=64)
+            nc.scalar.copy(
+                grouped[:].rearrange("p (c i) j -> p c j i", i=4),
+                h_raw[u][:].rearrange("p j (c i) -> p c j i", i=4),
+            )
+            code = keep.tile([P, HALF], U32, name="h_code%d" % u, align_bytes=64)
+            scale = keep.tile([P, HALF], U8, name="h_scale%d" % u, align_bytes=64)
+            nc.vector.quantize_mx(out=code[:].bitcast(FP8X4), scales=scale[:], in_=grouped[:].rearrange("p c j -> p (c j)"))
+            h_code.append(code)
+            h_scale.append(scale)
+
+        quantize_half(0)
+        x_code = []
+        for b in range(S // N):
+            picked = keep.tile([P, N], U32, name="x_code%d" % b, align_bytes=64)
+            nc.vector.tensor_copy(picked[:], word_table[:].bitcast(U32).indirect(offsets[:, b * N // 16 : (b + 1) * N // 16]))
+            x_code.append(picked)
+        quantize_half(1)
+
+        def scores(a, b):
+            u, c0 = divmod(a * P, HALF)
+            bank = psum.tile([P, N], F32, name="bank%d_%d" % (a, b))
+            nc.tensor.matmul_mx(
+                out=bank[:],
+                lhsT=h_code[u][:, c0 : c0 + P].bitcast(FP8X4),
+                lhsT_scale=h_scale[u][:, c0 : c0 + P],
+                rhs=x_code[b][:].bitcast(FP8X4),
+                rhs_scale=x_scale[:, b * N : (b + 1) * N],
+                start=True,
+                stop=True,
+            )
+            return bank
+
+        docs = N // D
+        banks = {}
+        for a, b in ((0, 0), (1, 0), (0, 1), (1, 1), (2, 0), (2, 1), (3, 0), (3, 1)):
+            banks[a, b] = scores(a, b)
+
+        best = [keep.tile([P, G], F32, name="best%d" % a) for a in range(2)]
+        for a, b in ((0, 0), (1, 0), (0, 1), (1, 1)):
+            nc.vector.tensor_reduce(best[a][:, b * docs : (b + 1) * docs], banks[a, b][:].rearrange("p (v d) -> p v d", d=D), AXIS_X, MAX)
+        for a in range(2):
+            result = keep.tile([P, G], F32, name="result%d" % a)
+            nc.scalar.activation(result[:], best[a][:], SIGMOID)
+            nc.sync.dma_start(out[a * P : (a + 1) * P, :], result[:])
+        for a in range(2, 4):
+            result = keep.tile([P, G], F32, name="result%d" % a)
+            for b in range(2):
+                squashed = keep.tile([P, N], F32, name="squashed%d_%d" % (a, b))
+                nc.scalar.activation(squashed[:], banks[a, b][:], SIGMOID)
+                nc.vector.tensor_reduce(result[:, b * docs : (b + 1) * docs], squashed[:].rearrange("p (v d) -> p v d", d=D), AXIS_X, MAX)
+            nc.sync.dma_start(out[a * P : (a + 1) * P, :], result[:])

@@ -19,7 +19,9 @@ AXIS_X = mybir.AxisListType.X
 P = 128
 PACK = 4
 N = 512
-HALF = 256
+CHUNKS = ((0, 128), (128, 256), (256, 384), (384, 512))
+WORDS_AHEAD = 256
+FIRST_PICK = 512
 
 
 def tile_picked_zlate_sig_p_kernel(tc, x_words, x_scales, hT, offs, out):
@@ -31,56 +33,63 @@ def tile_picked_zlate_sig_p_kernel(tc, x_words, x_scales, hT, offs, out):
         offsets = keep.tile([P, S // 16], U16, name="offsets")
         nc.sync.dma_start(offsets[:], offs)
 
+        word_rows = x_words[0].rearrange("p n r -> p (n r)").bitcast(I32)
+        word_table = keep.tile([P, T], I32, name="word_table", align_bytes=64)
+        nc.sync.dma_start(word_table[:, :WORDS_AHEAD], word_rows[:, :WORDS_AHEAD])
+
         scale_table = keep.tile([P, T], U8, name="scale_table", align_bytes=64)
-        nc.vector.memset(scale_table[:].bitcast(I32), 0)
+        nc.vector.memset(scale_table[:, : T // 2].bitcast(I32), 0)
+        nc.gpsimd.memset(scale_table[:, T // 2 :].bitcast(I32), 0)
         for q in range(4):
-            nc.scalar.dma_start(scale_table[32 * q : 32 * q + 4, :].bitcast(I32), x_scales[0, 4 * q : 4 * q + 4, :].bitcast(I32))
+            (nc.sync, nc.scalar)[q % 2].dma_start(scale_table[32 * q : 32 * q + 4, :].bitcast(I32), x_scales[0, 4 * q : 4 * q + 4, :].bitcast(I32))
+
+        nc.sync.dma_start(word_table[:, WORDS_AHEAD:], word_rows[:, WORDS_AHEAD:])
+        h_rows = hT.rearrange("(p j) c -> p j c", j=PACK)
+        h_raw = [keep.tile([P, PACK, c1 - c0], F32, name="h_raw%d" % c0) for c0, c1 in CHUNKS]
+        for u in range(len(CHUNKS)):
+            nc.sync.dma_start(h_raw[u][:], h_rows[:, :, CHUNKS[u][0] : CHUNKS[u][1]])
 
         warm_in = keep.tile([P, 1], F32, name="warm_in")
         warm_out = keep.tile([P, 1], F32, name="warm_out")
         nc.vector.memset(warm_in[:], 0.0)
         nc.scalar.activation(warm_out[:], warm_in[:], SIGMOID)
 
-        h_rows = hT.rearrange("(p j) c -> p j c", j=PACK)
-        h_raw = [keep.tile([P, PACK, HALF], F32, name="h_raw%d" % u) for u in range(2)]
-        word_table = keep.tile([P, T], I32, name="word_table", align_bytes=64)
-        nc.sync.dma_start(h_raw[0][:], h_rows[:, :, 0:HALF])
-        nc.sync.dma_start(word_table[:], x_words[0].rearrange("p n r -> p (n r)").bitcast(I32))
-        nc.sync.dma_start(h_raw[1][:], h_rows[:, :, HALF : 2 * HALF])
-
         x_scale = keep.tile([P, S], U8, name="x_scale", align_bytes=64)
         nc.vector.tensor_copy(x_scale[:], scale_table[:].indirect(offsets[:]))
 
-        h_code = []
-        h_scale = []
+        h_code = {}
+        h_scale = {}
 
-        def quantize_half(u):
-            grouped = keep.tile([P, HALF, PACK], BF16, name="grouped%d" % u, align_bytes=64)
+        def quantize_chunk(u):
+            c0, c1 = CHUNKS[u]
+            grouped = keep.tile([P, c1 - c0, PACK], BF16, name="grouped%d" % u, tag="shared%d" % u, align_bytes=64)
             nc.scalar.copy(
                 grouped[:].rearrange("p (c i) j -> p c j i", i=4),
                 h_raw[u][:].rearrange("p j (c i) -> p c j i", i=4),
             )
-            code = keep.tile([P, HALF], U32, name="h_code%d" % u, align_bytes=64)
-            scale = keep.tile([P, HALF], U8, name="h_scale%d" % u, align_bytes=64)
+            code = keep.tile([P, c1 - c0], U32, name="h_code%d" % u, align_bytes=64)
+            scale = keep.tile([P, c1 - c0], U8, name="h_scale%d" % u, align_bytes=64)
             nc.vector.quantize_mx(out=code[:].bitcast(FP8X4), scales=scale[:], in_=grouped[:].rearrange("p c j -> p (c j)"))
-            h_code.append(code)
-            h_scale.append(scale)
+            for a in range(c0 // P, c1 // P):
+                h_code[a] = code[:, a * P - c0 : (a + 1) * P - c0]
+                h_scale[a] = scale[:, a * P - c0 : (a + 1) * P - c0]
 
-        quantize_half(0)
         x_code = []
         for b in range(S // N):
-            picked = keep.tile([P, N], U32, name="x_code%d" % b, align_bytes=64)
+            picked = keep.tile([P, N], U32, name="x_code%d" % b, tag="shared0" if b == 1 else "x_code0", align_bytes=64)
             nc.vector.tensor_copy(picked[:], word_table[:].bitcast(U32).indirect(offsets[:, b * N // 16 : (b + 1) * N // 16]))
             x_code.append(picked)
-        quantize_half(1)
+            if b == 0:
+                quantize_chunk(0)
+        for u in range(1, len(CHUNKS)):
+            quantize_chunk(u)
 
         def scores(a, b):
-            u, c0 = divmod(a * P, HALF)
             bank = psum.tile([P, N], F32, name="bank%d_%d" % (a, b))
             nc.tensor.matmul_mx(
                 out=bank[:],
-                lhsT=h_code[u][:, c0 : c0 + P].bitcast(FP8X4),
-                lhsT_scale=h_scale[u][:, c0 : c0 + P],
+                lhsT=h_code[a].bitcast(FP8X4),
+                lhsT_scale=h_scale[a],
                 rhs=x_code[b][:].bitcast(FP8X4),
                 rhs_scale=x_scale[:, b * N : (b + 1) * N],
                 start=True,
@@ -89,21 +98,18 @@ def tile_picked_zlate_sig_p_kernel(tc, x_words, x_scales, hT, offs, out):
             return bank
 
         docs = N // D
-        banks = {}
-        for a, b in ((0, 0), (1, 0), (0, 1), (1, 1), (2, 0), (2, 1), (3, 0), (3, 1)):
-            banks[a, b] = scores(a, b)
-
-        best = [keep.tile([P, G], F32, name="best%d" % a) for a in range(2)]
-        for a, b in ((0, 0), (1, 0), (0, 1), (1, 1)):
-            nc.vector.tensor_reduce(best[a][:, b * docs : (b + 1) * docs], banks[a, b][:].rearrange("p (v d) -> p v d", d=D), AXIS_X, MAX)
-        for a in range(2):
+        hold = {(0, 0): "shared1", (0, 1): "shared2", (1, 0): "shared3"}
+        for a in range(J // P):
+            banks = [scores(a, b) for b in range(S // N)]
             result = keep.tile([P, G], F32, name="result%d" % a)
-            nc.scalar.activation(result[:], best[a][:], SIGMOID)
-            nc.sync.dma_start(out[a * P : (a + 1) * P, :], result[:])
-        for a in range(2, 4):
-            result = keep.tile([P, G], F32, name="result%d" % a)
-            for b in range(2):
-                squashed = keep.tile([P, N], F32, name="squashed%d_%d" % (a, b))
-                nc.scalar.activation(squashed[:], banks[a, b][:], SIGMOID)
-                nc.vector.tensor_reduce(result[:, b * docs : (b + 1) * docs], squashed[:].rearrange("p (v d) -> p v d", d=D), AXIS_X, MAX)
+            for b in range(S // N):
+                cols = slice(b * docs, (b + 1) * docs)
+                if a < 3:
+                    best = keep.tile([P, docs], F32, name="best%d_%d" % (a, b), tag=hold.get((a, b), "best%d_%d" % (a, b)), align_bytes=64)
+                    nc.vector.tensor_reduce(best[:], banks[b][:].rearrange("p (v d) -> p v d", d=D), AXIS_X, MAX)
+                    nc.scalar.activation(result[:, cols], best[:], SIGMOID)
+                else:
+                    squashed = keep.tile([P, N], F32, name="squashed%d_%d" % (a, b))
+                    nc.scalar.activation(squashed[:], banks[b][:], SIGMOID)
+                    nc.vector.tensor_reduce(result[:, cols], squashed[:].rearrange("p (v d) -> p v d", d=D), AXIS_X, MAX)
             nc.sync.dma_start(out[a * P : (a + 1) * P, :], result[:])

@@ -20,8 +20,9 @@ P = 128
 PACK = 4
 N = 512
 CHUNKS = ((0, 128), (128, 256), (256, 384), (384, 512))
-WORDS_AHEAD = 256
-FIRST_PICK = 512
+WORDS_AHEAD = 64
+PASSES = ((0, 512), (512, 640), (640, 768), (768, 1024))
+PICKS = ((0, 640), (640, 1024))
 
 
 def tile_picked_zlate_sig_p_kernel(tc, x_words, x_scales, hT, offs, out):
@@ -35,11 +36,11 @@ def tile_picked_zlate_sig_p_kernel(tc, x_words, x_scales, hT, offs, out):
 
         word_rows = x_words[0].rearrange("p n r -> p (n r)").bitcast(I32)
         word_table = keep.tile([P, T], I32, name="word_table", align_bytes=64)
-        nc.sync.dma_start(word_table[:, :WORDS_AHEAD], word_rows[:, :WORDS_AHEAD])
+        if WORDS_AHEAD:
+            nc.sync.dma_start(word_table[:, :WORDS_AHEAD], word_rows[:, :WORDS_AHEAD])
 
         scale_table = keep.tile([P, T], U8, name="scale_table", align_bytes=64)
-        nc.vector.memset(scale_table[:, : T // 2].bitcast(I32), 0)
-        nc.gpsimd.memset(scale_table[:, T // 2 :].bitcast(I32), 0)
+        nc.vector.memset(scale_table[:].bitcast(I32), 0)
         for q in range(4):
             (nc.sync, nc.scalar)[q % 2].dma_start(scale_table[32 * q : 32 * q + 4, :].bitcast(I32), x_scales[0, 4 * q : 4 * q + 4, :].bitcast(I32))
 
@@ -60,45 +61,46 @@ def tile_picked_zlate_sig_p_kernel(tc, x_words, x_scales, hT, offs, out):
         h_code = {}
         h_scale = {}
 
-        def quantize_chunk(u):
-            c0, c1 = CHUNKS[u]
-            grouped = keep.tile([P, c1 - c0, PACK], BF16, name="grouped%d" % u, tag="shared%d" % u, align_bytes=64)
+        def quantize_tile(a):
+            u = [i for i, (c0, c1) in enumerate(CHUNKS) if c0 <= a * P < c1][0]
+            c0 = a * P - CHUNKS[u][0]
+            grouped = keep.tile([P, P, PACK], BF16, name="grouped%d" % a, tag="shared%d" % a, align_bytes=64)
             nc.scalar.copy(
                 grouped[:].rearrange("p (c i) j -> p c j i", i=4),
-                h_raw[u][:].rearrange("p j (c i) -> p c j i", i=4),
+                h_raw[u][:, :, c0 : c0 + P].rearrange("p j (c i) -> p c j i", i=4),
             )
-            code = keep.tile([P, c1 - c0], U32, name="h_code%d" % u, align_bytes=64)
-            scale = keep.tile([P, c1 - c0], U8, name="h_scale%d" % u, align_bytes=64)
-            nc.vector.quantize_mx(out=code[:].bitcast(FP8X4), scales=scale[:], in_=grouped[:].rearrange("p c j -> p (c j)"))
-            for a in range(c0 // P, c1 // P):
-                h_code[a] = code[:, a * P - c0 : (a + 1) * P - c0]
-                h_scale[a] = scale[:, a * P - c0 : (a + 1) * P - c0]
+            h_code[a] = keep.tile([P, P], U32, name="h_code%d" % a, align_bytes=64)
+            h_scale[a] = keep.tile([P, P], U8, name="h_scale%d" % a, align_bytes=64)
+            nc.vector.quantize_mx(out=h_code[a][:].bitcast(FP8X4), scales=h_scale[a][:], in_=grouped[:].rearrange("p c j -> p (c j)"))
 
         x_code = []
-        for b in range(S // N):
-            picked = keep.tile([P, N], U32, name="x_code%d" % b, tag="shared0" if b == 1 else "x_code0", align_bytes=64)
-            nc.vector.tensor_copy(picked[:], word_table[:].bitcast(U32).indirect(offsets[:, b * N // 16 : (b + 1) * N // 16]))
+        for i, (j0, j1) in enumerate(PICKS):
+            if i == len(PICKS) - 1:
+                quantize_tile(0)
+            picked = keep.tile([P, j1 - j0], U32, name="x_code%d" % i, tag="shared0" if i == len(PICKS) - 1 else "x_code%d" % i, align_bytes=64)
+            nc.vector.tensor_copy(picked[:], word_table[:].bitcast(U32).indirect(offsets[:, j0 // 16 : j1 // 16]))
             x_code.append(picked)
-            if b == 0:
-                quantize_chunk(0)
-        for u in range(1, len(CHUNKS)):
-            quantize_chunk(u)
+        for a in range(1, J // P):
+            quantize_tile(a)
 
         def scores(a, b):
             bank = psum.tile([P, N], F32, name="bank%d_%d" % (a, b))
-            nc.tensor.matmul_mx(
-                out=bank[:],
-                lhsT=h_code[a].bitcast(FP8X4),
-                lhsT_scale=h_scale[a],
-                rhs=x_code[b][:].bitcast(FP8X4),
-                rhs_scale=x_scale[:, b * N : (b + 1) * N],
-                start=True,
-                stop=True,
-            )
+            for j0, j1 in PASSES:
+                if j0 // N == b:
+                    i = [n for n, (p0, p1) in enumerate(PICKS) if p0 <= j0 < p1][0]
+                    nc.tensor.matmul_mx(
+                        out=bank[:, j0 - b * N : j1 - b * N],
+                        lhsT=h_code[a][:].bitcast(FP8X4),
+                        lhsT_scale=h_scale[a][:],
+                        rhs=x_code[i][:, j0 - PICKS[i][0] : j1 - PICKS[i][0]].bitcast(FP8X4),
+                        rhs_scale=x_scale[:, j0:j1],
+                        start=True,
+                        stop=True,
+                    )
             return bank
 
         docs = N // D
-        hold = {(0, 0): "shared1", (0, 1): "shared2", (1, 0): "shared3"}
+        hold = {(0, 0): "shared1", (1, 0): "shared2", (1, 1): "shared3"}
         for a in range(J // P):
             banks = [scores(a, b) for b in range(S // N)]
             result = keep.tile([P, G], F32, name="result%d" % a)

@@ -20,7 +20,7 @@ P = 128
 PACK = 4
 N = 512
 CHUNKS = ((0, 128), (128, 256), (256, 384), (384, 512))
-WORDS_AHEAD = 64
+WORDS_AHEAD = 256
 PASSES = ((0, 512), (512, 640), (640, 768), (768, 1024))
 PICKS = ((0, 640), (640, 1024))
 
@@ -42,7 +42,7 @@ def tile_picked_zlate_sig_p_kernel(tc, x_words, x_scales, hT, offs, out):
         scale_table = keep.tile([P, T], U8, name="scale_table", align_bytes=64)
         nc.vector.memset(scale_table[:].bitcast(I32), 0)
         for q in range(4):
-            (nc.sync, nc.scalar)[q % 2].dma_start(scale_table[32 * q : 32 * q + 4, :].bitcast(I32), x_scales[0, 4 * q : 4 * q + 4, :].bitcast(I32))
+            (nc.sync, nc.scalar)[q % 2].dma_start(scale_table[q:P:32, :].bitcast(I32), x_scales[0, q:16:4, :].bitcast(I32))
 
         nc.sync.dma_start(word_table[:, WORDS_AHEAD:], word_rows[:, WORDS_AHEAD:])
         h_rows = hT.rearrange("(p j) c -> p j c", j=PACK)
@@ -100,7 +100,7 @@ def tile_picked_zlate_sig_p_kernel(tc, x_words, x_scales, hT, offs, out):
             return bank
 
         docs = N // D
-        hold = {(0, 0): "shared1", (1, 0): "shared2", (1, 1): "shared3"}
+        hold = {(1, 0): "shared2", (1, 1): "shared3"}
         for a in range(J // P):
             banks = [scores(a, b) for b in range(S // N)]
             result = keep.tile([P, G], F32, name="result%d" % a)

@@ -21,8 +21,8 @@ PACK = 4
 N = 512
 CHUNKS = ((0, 128), (128, 256), (256, 384), (384, 512))
 WORDS_AHEAD = 256
-PASSES = ((0, 512), (512, 640), (640, 768), (768, 1024))
-PICKS = ((0, 640), (640, 1024))
+PASSES = ((0, 512), (512, 1024))
+PICKS = ((0, 512), (512, 1024))
 
 
 def tile_picked_zlate_sig_p_kernel(tc, x_words, x_scales, hT, offs, out):
@@ -42,11 +42,11 @@ def tile_picked_zlate_sig_p_kernel(tc, x_words, x_scales, hT, offs, out):
         scale_table = keep.tile([P, T], U8, name="scale_table", align_bytes=64)
         nc.vector.memset(scale_table[:].bitcast(I32), 0)
         for q in range(4):
-            (nc.sync, nc.scalar)[q % 2].dma_start(scale_table[q:P:32, :].bitcast(I32), x_scales[0, q:16:4, :].bitcast(I32))
+            nc.sync.dma_start(scale_table[q:P:32, :].bitcast(I32), x_scales[0, q:16:4, :].bitcast(I32))
 
         nc.sync.dma_start(word_table[:, WORDS_AHEAD:], word_rows[:, WORDS_AHEAD:])
         h_rows = hT.rearrange("(p j) c -> p j c", j=PACK)
-        h_raw = [keep.tile([P, PACK, c1 - c0], F32, name="h_raw%d" % c0) for c0, c1 in CHUNKS]
+        h_raw = [keep.tile([P, PACK, c1 - c0], F32, name="h_raw%d" % c0, align_bytes=64) for c0, c1 in CHUNKS]
         for u in range(len(CHUNKS)):
             nc.sync.dma_start(h_raw[u][:], h_rows[:, :, CHUNKS[u][0] : CHUNKS[u][1]])
 
@@ -77,7 +77,7 @@ def tile_picked_zlate_sig_p_kernel(tc, x_words, x_scales, hT, offs, out):
         for i, (j0, j1) in enumerate(PICKS):
             if i == len(PICKS) - 1:
                 quantize_tile(0)
-            picked = keep.tile([P, j1 - j0], U32, name="x_code%d" % i, tag="shared0" if i == len(PICKS) - 1 else "x_code%d" % i, align_bytes=64)
+            picked = keep.tile([P, j1 - j0], U32, name="x_code%d" % i, tag="h_raw0" if i == len(PICKS) - 1 else "x_code%d" % i, align_bytes=64)
             nc.vector.tensor_copy(picked[:], word_table[:].bitcast(U32).indirect(offsets[:, j0 // 16 : j1 // 16]))
             x_code.append(picked)
         for a in range(1, J // P):
@@ -101,17 +101,19 @@ def tile_picked_zlate_sig_p_kernel(tc, x_words, x_scales, hT, offs, out):
 
         docs = N // D
         hold = {(1, 0): "shared2", (1, 1): "shared3"}
+        last = J // P - 1
         for a in range(J // P):
-            banks = [scores(a, b) for b in range(S // N)]
             result = keep.tile([P, G], F32, name="result%d" % a)
+            if a == last:
+                squashed = keep.tile([P, N], F32, name="squashed")
+                nc.scalar.activation(squashed[:], scores(a, 1)[:], SIGMOID)
             for b in range(S // N):
                 cols = slice(b * docs, (b + 1) * docs)
-                if a < 3:
+                if (a, b) != (last, 1):
+                    bank = scores(a, b)
                     best = keep.tile([P, docs], F32, name="best%d_%d" % (a, b), tag=hold.get((a, b), "best%d_%d" % (a, b)), align_bytes=64)
-                    nc.vector.tensor_reduce(best[:], banks[b][:].rearrange("p (v d) -> p v d", d=D), AXIS_X, MAX)
+                    nc.vector.tensor_reduce(best[:], bank[:].rearrange("p (v d) -> p v d", d=D), AXIS_X, MAX)
                     nc.scalar.activation(result[:, cols], best[:], SIGMOID)
                 else:
-                    squashed = keep.tile([P, N], F32, name="squashed%d_%d" % (a, b))
-                    nc.scalar.activation(squashed[:], banks[b][:], SIGMOID)
                     nc.vector.tensor_reduce(result[:, cols], squashed[:].rearrange("p (v d) -> p v d", d=D), AXIS_X, MAX)
             nc.sync.dma_start(out[a * P : (a + 1) * P, :], result[:])

@@ -21,8 +21,8 @@ PACK = 4
 N = 512
 CHUNKS = ((0, 128), (128, 256), (256, 384), (384, 512))
 WORDS_AHEAD = 256
-PASSES = ((0, 512), (512, 1024))
-PICKS = ((0, 512), (512, 1024))
+PASSES = ((0, 512), (512, 640), (640, 768), (768, 1024))
+PICKS = ((0, 640), (640, 1024))
 
 
 def tile_picked_zlate_sig_p_kernel(tc, x_words, x_scales, hT, offs, out):
@@ -49,11 +49,6 @@ def tile_picked_zlate_sig_p_kernel(tc, x_words, x_scales, hT, offs, out):
         h_raw = [keep.tile([P, PACK, c1 - c0], F32, name="h_raw%d" % c0, align_bytes=64) for c0, c1 in CHUNKS]
         for u in range(len(CHUNKS)):
             nc.sync.dma_start(h_raw[u][:], h_rows[:, :, CHUNKS[u][0] : CHUNKS[u][1]])
-
-        warm_in = keep.tile([P, 1], F32, name="warm_in")
-        warm_out = keep.tile([P, 1], F32, name="warm_out")
-        nc.vector.memset(warm_in[:], 0.0)
-        nc.scalar.activation(warm_out[:], warm_in[:], SIGMOID)
 
         x_scale = keep.tile([P, S], U8, name="x_scale", align_bytes=64)
         nc.vector.tensor_copy(x_scale[:], scale_table[:].indirect(offsets[:]))
@@ -116,4 +111,7 @@ def tile_picked_zlate_sig_p_kernel(tc, x_words, x_scales, hT, offs, out):
                     nc.scalar.activation(result[:, cols], best[:], SIGMOID)
                 else:
                     nc.vector.tensor_reduce(result[:, cols], squashed[:].rearrange("p (v d) -> p v d", d=D), AXIS_X, MAX)
-            nc.sync.dma_start(out[a * P : (a + 1) * P, :], result[:])
+                if a == last:
+                    nc.sync.dma_start(out[a * P : (a + 1) * P, cols], result[:, cols])
+            if a != last:
+                nc.sync.dma_start(out[a * P : (a + 1) * P, :], result[:])

@@ -20,7 +20,7 @@ P = 128
 PACK = 4
 N = 512
 CHUNKS = ((0, 128), (128, 256), (256, 384), (384, 512))
-WORDS_AHEAD = 256
+WORDS_AHEAD = 384
 PASSES = ((0, 512), (512, 640), (640, 768), (768, 1024))
 PICKS = ((0, 640), (640, 1024))
 
@@ -32,12 +32,11 @@ def tile_picked_zlate_sig_p_kernel(tc, x_words, x_scales, hT, offs, out):
         psum = ctx.enter_context(tc.psum_pool(name="psum", bufs=1))
 
         offsets = keep.tile([P, S // 16], U16, name="offsets")
-        nc.sync.dma_start(offsets[:], offs)
 
         word_rows = x_words[0].rearrange("p n r -> p (n r)").bitcast(I32)
         word_table = keep.tile([P, T], I32, name="word_table", align_bytes=64)
-        if WORDS_AHEAD:
-            nc.sync.dma_start(word_table[:, :WORDS_AHEAD], word_rows[:, :WORDS_AHEAD])
+        nc.sync.dma_start(word_table[:, :WORDS_AHEAD], word_rows[:, :WORDS_AHEAD])
+        nc.sync.dma_start(offsets[:], offs)
 
         scale_table = keep.tile([P, T], U8, name="scale_table", align_bytes=64)
         nc.vector.memset(scale_table[:].bitcast(I32), 0)

@@ -19,10 +19,9 @@ AXIS_X = mybir.AxisListType.X
 P = 128
 PACK = 4
 N = 512
-CHUNKS = ((0, 128), (128, 256), (256, 384), (384, 512))
+TILES = J // P
 WORDS_AHEAD = 384
-PASSES = ((0, 512), (512, 640), (640, 768), (768, 1024))
-PICKS = ((0, 640), (640, 1024))
+FIRST = 640
 
 
 def tile_picked_zlate_sig_p_kernel(tc, x_words, x_scales, hT, offs, out):
@@ -45,72 +44,80 @@ def tile_picked_zlate_sig_p_kernel(tc, x_words, x_scales, hT, offs, out):
 
         nc.sync.dma_start(word_table[:, WORDS_AHEAD:], word_rows[:, WORDS_AHEAD:])
         h_rows = hT.rearrange("(p j) c -> p j c", j=PACK)
-        h_raw = [keep.tile([P, PACK, c1 - c0], F32, name="h_raw%d" % c0, align_bytes=64) for c0, c1 in CHUNKS]
-        for u in range(len(CHUNKS)):
-            nc.sync.dma_start(h_raw[u][:], h_rows[:, :, CHUNKS[u][0] : CHUNKS[u][1]])
+        h_raw = [keep.tile([P, PACK, P], F32, name="h_raw%d" % a, align_bytes=64) for a in range(TILES)]
+        for a in range(TILES):
+            nc.sync.dma_start(h_raw[a][:], h_rows[:, :, a * P : (a + 1) * P])
 
         x_scale = keep.tile([P, S], U8, name="x_scale", align_bytes=64)
         nc.vector.tensor_copy(x_scale[:], scale_table[:].indirect(offsets[:]))
+
+        grouped = [keep.tile([P, P, PACK], BF16, name="grouped%d" % a, align_bytes=64) for a in range(TILES)]
+        for a in range(TILES):
+            nc.scalar.copy(
+                grouped[a][:].rearrange("p (c i) j -> p c j i", i=4),
+                h_raw[a][:].rearrange("p j (c i) -> p c j i", i=4),
+            )
 
         h_code = {}
         h_scale = {}
 
         def quantize_tile(a):
-            u = [i for i, (c0, c1) in enumerate(CHUNKS) if c0 <= a * P < c1][0]
-            c0 = a * P - CHUNKS[u][0]
-            grouped = keep.tile([P, P, PACK], BF16, name="grouped%d" % a, tag="shared%d" % a, align_bytes=64)
-            nc.scalar.copy(
-                grouped[:].rearrange("p (c i) j -> p c j i", i=4),
-                h_raw[u][:, :, c0 : c0 + P].rearrange("p j (c i) -> p c j i", i=4),
-            )
-            h_code[a] = keep.tile([P, P], U32, name="h_code%d" % a, align_bytes=64)
+            h_code[a] = keep.tile([P, P], U32, name="h_code%d" % a, tag="h_code%d" % (a % 2), align_bytes=64)
             h_scale[a] = keep.tile([P, P], U8, name="h_scale%d" % a, align_bytes=64)
-            nc.vector.quantize_mx(out=h_code[a][:].bitcast(FP8X4), scales=h_scale[a][:], in_=grouped[:].rearrange("p c j -> p (c j)"))
+            nc.vector.quantize_mx(out=h_code[a][:].bitcast(FP8X4), scales=h_scale[a][:], in_=grouped[a][:].rearrange("p c j -> p (c j)"))
 
-        x_code = []
-        for i, (j0, j1) in enumerate(PICKS):
-            if i == len(PICKS) - 1:
-                quantize_tile(0)
-            picked = keep.tile([P, j1 - j0], U32, name="x_code%d" % i, tag="h_raw0" if i == len(PICKS) - 1 else "x_code%d" % i, align_bytes=64)
-            nc.vector.tensor_copy(picked[:], word_table[:].bitcast(U32).indirect(offsets[:, j0 // 16 : j1 // 16]))
-            x_code.append(picked)
-        for a in range(1, J // P):
-            quantize_tile(a)
+        first_code = keep.tile([P, FIRST], U32, name="first_code", align_bytes=64)
+        nc.vector.tensor_copy(first_code[:], word_table[:].bitcast(U32).indirect(offsets[:, : FIRST // 16]))
+        quantize_tile(0)
+        rest_code = keep.tile([P, S - FIRST], U32, name="rest_code", tag="h_raw0", align_bytes=64)
+        nc.vector.tensor_copy(rest_code[:], word_table[:].bitcast(U32).indirect(offsets[:, FIRST // 16 :]))
+        quantize_tile(1)
 
-        def scores(a, b):
-            bank = psum.tile([P, N], F32, name="bank%d_%d" % (a, b))
-            for j0, j1 in PASSES:
-                if j0 // N == b:
-                    i = [n for n, (p0, p1) in enumerate(PICKS) if p0 <= j0 < p1][0]
-                    nc.tensor.matmul_mx(
-                        out=bank[:, j0 - b * N : j1 - b * N],
-                        lhsT=h_code[a][:].bitcast(FP8X4),
-                        lhsT_scale=h_scale[a][:],
-                        rhs=x_code[i][:, j0 - PICKS[i][0] : j1 - PICKS[i][0]].bitcast(FP8X4),
-                        rhs_scale=x_scale[:, j0:j1],
-                        start=True,
-                        stop=True,
-                    )
-            return bank
+        def scores(a, spans, tag):
+            base = spans[0][0]
+            bank = psum.tile([P, N], F32, name="bank%d_%d" % (a, base), tag=tag)
+            for j0, j1 in spans:
+                codes = first_code[:, j0:j1] if j1 <= FIRST else rest_code[:, j0 - FIRST : j1 - FIRST]
+                nc.tensor.matmul_mx(
+                    out=bank[:, j0 - base : j1 - base],
+                    lhsT=h_code[a][:].bitcast(FP8X4),
+                    lhsT_scale=h_scale[a][:],
+                    rhs=codes.bitcast(FP8X4),
+                    rhs_scale=x_scale[:, j0:j1],
+                    start=True,
+                    stop=True,
+                )
+            return bank[:, : spans[-1][1] - base]
 
-        docs = N // D
-        hold = {(1, 0): "shared2", (1, 1): "shared3"}
-        last = J // P - 1
-        for a in range(J // P):
-            result = keep.tile([P, G], F32, name="result%d" % a)
-            if a == last:
-                squashed = keep.tile([P, N], F32, name="squashed")
-                nc.scalar.activation(squashed[:], scores(a, 1)[:], SIGMOID)
-            for b in range(S // N):
-                cols = slice(b * docs, (b + 1) * docs)
-                if (a, b) != (last, 1):
-                    bank = scores(a, b)
-                    best = keep.tile([P, docs], F32, name="best%d_%d" % (a, b), tag=hold.get((a, b), "best%d_%d" % (a, b)), align_bytes=64)
-                    nc.vector.tensor_reduce(best[:], bank[:].rearrange("p (v d) -> p v d", d=D), AXIS_X, MAX)
-                    nc.scalar.activation(result[:, cols], best[:], SIGMOID)
-                else:
-                    nc.vector.tensor_reduce(result[:, cols], squashed[:].rearrange("p (v d) -> p v d", d=D), AXIS_X, MAX)
-                if a == last:
-                    nc.sync.dma_start(out[a * P : (a + 1) * P, cols], result[:, cols])
-            if a != last:
-                nc.sync.dma_start(out[a * P : (a + 1) * P, :], result[:])
+        def by_doc(t):
+            return t.rearrange("p (v d) -> p v d", d=D)
+
+        low = ((0, N),)
+        high = ((N, FIRST), (FIRST, 768), (768, S))
+        half = G // 2
+        best = [keep.tile([P, G], F32, name="best%d" % a, tag=t, align_bytes=64) for a, t in enumerate(("best0", "best1", "best2", "best3"))]
+        result = [keep.tile([P, G], F32, name="result%d" % a) for a in range(TILES)]
+
+        def finish(a, c0, c1):
+            nc.scalar.activation(result[a][:, c0:c1], best[a][:, c0:c1], SIGMOID)
+            nc.sync.dma_start(out[a * P : (a + 1) * P, c0:c1], result[a][:, c0:c1])
+
+        nc.vector.tensor_reduce(best[0][:, :half], by_doc(scores(0, low, "b0")), AXIS_X, MAX)
+        for n, spans in enumerate((high[:1], high[1:])):
+            nc.vector.tensor_reduce(best[0][:, spans[0][0] // D : spans[-1][1] // D], by_doc(scores(0, spans, "b%d" % (1 + n))), AXIS_X, MAX)
+        finish(0, 0, G)
+        quantize_tile(2)
+        nc.vector.tensor_reduce(best[1][:, :half], by_doc(scores(1, low, "b3")), AXIS_X, MAX)
+        bank = scores(1, high, "b4")
+        quantize_tile(3)
+        nc.vector.tensor_reduce(best[1][:, half:], by_doc(bank), AXIS_X, MAX)
+        finish(1, 0, G)
+        nc.vector.tensor_reduce(best[2][:, :half], by_doc(scores(2, low, "b5")), AXIS_X, MAX)
+        nc.vector.tensor_reduce(best[2][:, half:], by_doc(scores(2, high, "b6")), AXIS_X, MAX)
+        squashed = keep.tile([P, N], F32, name="squashed")
+        nc.scalar.activation(squashed[:], scores(3, high, "b7"), SIGMOID)
+        finish(2, 0, G)
+        nc.vector.tensor_reduce(best[3][:, :half], by_doc(scores(3, low, "b0")), AXIS_X, MAX)
+        finish(3, 0, half)
+        nc.vector.tensor_reduce(result[3][:, half:], by_doc(squashed[:]), AXIS_X, MAX)
+        nc.sync.dma_start(out[3 * P :, half:], result[3][:, half:])

@@ -62,7 +62,7 @@ def tile_picked_zlate_sig_p_kernel(tc, x_words, x_scales, hT, offs, out):
         h_scale = {}
 
         def quantize_tile(a):
-            h_code[a] = keep.tile([P, P], U32, name="h_code%d" % a, tag="h_code%d" % (a % 2), align_bytes=64)
+            h_code[a] = keep.tile([P, P], U32, name="h_code%d" % a, tag="h_code%d" % a, align_bytes=64)
             h_scale[a] = keep.tile([P, P], U8, name="h_scale%d" % a, align_bytes=64)
             nc.vector.quantize_mx(out=h_code[a][:].bitcast(FP8X4), scales=h_scale[a][:], in_=grouped[a][:].rearrange("p c j -> p (c j)"))
 
@@ -95,29 +95,31 @@ def tile_picked_zlate_sig_p_kernel(tc, x_words, x_scales, hT, offs, out):
         low = ((0, N),)
         high = ((N, FIRST), (FIRST, 768), (768, S))
         half = G // 2
-        best = [keep.tile([P, G], F32, name="best%d" % a, tag=t, align_bytes=64) for a, t in enumerate(("best0", "best1", "best2", "best3"))]
+        quantize_tile(2)
+        quantize_tile(3)
         result = [keep.tile([P, G], F32, name="result%d" % a) for a in range(TILES)]
 
-        def finish(a, c0, c1):
-            nc.scalar.activation(result[a][:, c0:c1], best[a][:, c0:c1], SIGMOID)
+        def reduce_banks(a, banks, tag):
+            c0, c1 = banks[0][0][0][0] // D, banks[-1][0][-1][1] // D
+            best = keep.tile([P, c1 - c0], F32, name="best%d_%d" % (a, c0), tag=tag, align_bytes=64)
+            for spans, bank in banks:
+                nc.vector.tensor_reduce(best[:, spans[0][0] // D - c0 : spans[-1][1] // D - c0], by_doc(scores(a, spans, bank)), AXIS_X, MAX)
+            nc.scalar.activation(result[a][:, c0:c1], best[:], SIGMOID)
+
+        def store(a, c0, c1):
             nc.sync.dma_start(out[a * P : (a + 1) * P, c0:c1], result[a][:, c0:c1])
 
-        nc.vector.tensor_reduce(best[0][:, :half], by_doc(scores(0, low, "b0")), AXIS_X, MAX)
-        for n, spans in enumerate((high[:1], high[1:])):
-            nc.vector.tensor_reduce(best[0][:, spans[0][0] // D : spans[-1][1] // D], by_doc(scores(0, spans, "b%d" % (1 + n))), AXIS_X, MAX)
-        finish(0, 0, G)
-        quantize_tile(2)
-        nc.vector.tensor_reduce(best[1][:, :half], by_doc(scores(1, low, "b3")), AXIS_X, MAX)
-        bank = scores(1, high, "b4")
-        quantize_tile(3)
-        nc.vector.tensor_reduce(best[1][:, half:], by_doc(bank), AXIS_X, MAX)
-        finish(1, 0, G)
-        nc.vector.tensor_reduce(best[2][:, :half], by_doc(scores(2, low, "b5")), AXIS_X, MAX)
-        nc.vector.tensor_reduce(best[2][:, half:], by_doc(scores(2, high, "b6")), AXIS_X, MAX)
+        reduce_banks(0, ((low, "b0"),), "best0")
+        reduce_banks(0, ((high[:2], "b1"), (high[2:], "b2")), "h_raw2")
+        store(0, 0, G)
+        reduce_banks(1, ((low, "b3"), (high, "b4")), "h_raw3")
+        store(1, 0, G)
+        reduce_banks(2, ((low, "b5"),), "best2")
         squashed = keep.tile([P, N], F32, name="squashed")
+        reduce_banks(2, ((high, "b6"),), "best3")
+        store(2, 0, G)
         nc.scalar.activation(squashed[:], scores(3, high, "b7"), SIGMOID)
-        finish(2, 0, G)
-        nc.vector.tensor_reduce(best[3][:, :half], by_doc(scores(3, low, "b0")), AXIS_X, MAX)
-        finish(3, 0, half)
+        reduce_banks(3, ((low, "b0"),), "best4")
+        store(3, 0, half)
         nc.vector.tensor_reduce(result[3][:, half:], by_doc(squashed[:]), AXIS_X, MAX)
-        nc.sync.dma_start(out[3 * P :, half:], result[3][:, half:])
+        store(3, half, G)

@@ -20,8 +20,11 @@ P = 128
 PACK = 4
 N = 512
 TILES = J // P
+GROUP = 16
+SCALE_ROWS = K // 32
 WORDS_AHEAD = 384
 FIRST = 640
+SECOND = 768
 
 
 def tile_picked_zlate_sig_p_kernel(tc, x_words, x_scales, hT, offs, out):
@@ -30,7 +33,7 @@ def tile_picked_zlate_sig_p_kernel(tc, x_words, x_scales, hT, offs, out):
         keep = ctx.enter_context(tc.tile_pool(name="keep", bufs=1))
         psum = ctx.enter_context(tc.psum_pool(name="psum", bufs=1))
 
-        offsets = keep.tile([P, S // 16], U16, name="offsets")
+        offsets = keep.tile([P, S // GROUP], U16, name="offsets")
 
         word_rows = x_words[0].rearrange("p n r -> p (n r)").bitcast(I32)
         word_table = keep.tile([P, T], I32, name="word_table", align_bytes=64)
@@ -40,7 +43,7 @@ def tile_picked_zlate_sig_p_kernel(tc, x_words, x_scales, hT, offs, out):
         scale_table = keep.tile([P, T], U8, name="scale_table", align_bytes=64)
         nc.vector.memset(scale_table[:].bitcast(I32), 0)
         for q in range(4):
-            nc.sync.dma_start(scale_table[q:P:32, :].bitcast(I32), x_scales[0, q:16:4, :].bitcast(I32))
+            nc.sync.dma_start(scale_table[q:P:32, :].bitcast(I32), x_scales[0, q:SCALE_ROWS:4, :].bitcast(I32))
 
         nc.sync.dma_start(word_table[:, WORDS_AHEAD:], word_rows[:, WORDS_AHEAD:])
         h_rows = hT.rearrange("(p j) c -> p j c", j=PACK)
@@ -62,15 +65,19 @@ def tile_picked_zlate_sig_p_kernel(tc, x_words, x_scales, hT, offs, out):
         h_scale = {}
 
         def quantize_tile(a):
-            h_code[a] = keep.tile([P, P], U32, name="h_code%d" % a, tag="h_code%d" % a, align_bytes=64)
+            h_code[a] = keep.tile([P, P], U32, name="h_code%d" % a, align_bytes=64)
             h_scale[a] = keep.tile([P, P], U8, name="h_scale%d" % a, align_bytes=64)
             nc.vector.quantize_mx(out=h_code[a][:].bitcast(FP8X4), scales=h_scale[a][:], in_=grouped[a][:].rearrange("p c j -> p (c j)"))
 
+        def gather_words(picked, j0, j1):
+            nc.vector.tensor_copy(picked, word_table[:].bitcast(U32).indirect(offsets[:, j0 // GROUP : j1 // GROUP]))
+
         first_code = keep.tile([P, FIRST], U32, name="first_code", align_bytes=64)
-        nc.vector.tensor_copy(first_code[:], word_table[:].bitcast(U32).indirect(offsets[:, : FIRST // 16]))
+        gather_words(first_code[:], 0, FIRST)
         quantize_tile(0)
         rest_code = keep.tile([P, S - FIRST], U32, name="rest_code", tag="h_raw0", align_bytes=64)
-        nc.vector.tensor_copy(rest_code[:], word_table[:].bitcast(U32).indirect(offsets[:, FIRST // 16 :]))
+        for j0, j1 in ((FIRST, SECOND), (SECOND, S)):
+            gather_words(rest_code[:, j0 - FIRST : j1 - FIRST], j0, j1)
         quantize_tile(1)
 
         def scores(a, spans, tag):
@@ -93,10 +100,8 @@ def tile_picked_zlate_sig_p_kernel(tc, x_words, x_scales, hT, offs, out):
             return t.rearrange("p (v d) -> p v d", d=D)
 
         low = ((0, N),)
-        high = ((N, FIRST), (FIRST, 768), (768, S))
+        high = ((N, FIRST), (FIRST, SECOND), (SECOND, S))
         half = G // 2
-        quantize_tile(2)
-        quantize_tile(3)
         result = [keep.tile([P, G], F32, name="result%d" % a) for a in range(TILES)]
 
         def reduce_banks(a, banks, tag):
@@ -110,8 +115,11 @@ def tile_picked_zlate_sig_p_kernel(tc, x_words, x_scales, hT, offs, out):
             nc.sync.dma_start(out[a * P : (a + 1) * P, c0:c1], result[a][:, c0:c1])
 
         reduce_banks(0, ((low, "b0"),), "best0")
-        reduce_banks(0, ((high[:2], "b1"), (high[2:], "b2")), "h_raw2")
+        reduce_banks(0, ((high[:2], "b1"),), "best1")
+        quantize_tile(2)
+        reduce_banks(0, ((high[2:], "b2"),), "h_raw2")
         store(0, 0, G)
+        quantize_tile(3)
         reduce_banks(1, ((low, "b3"), (high, "b4")), "h_raw3")
         store(1, 0, G)
         reduce_banks(2, ((low, "b5"),), "best2")

@@ -22,6 +22,7 @@ N = 512
 TILES = J // P
 GROUP = 16
 SCALE_ROWS = K // 32
+BURST = 256
 WORDS_AHEAD = 384
 FIRST = 640
 SECOND = 768
@@ -36,18 +37,18 @@ def tile_picked_zlate_sig_p_kernel(tc, x_words, x_scales, hT, offs, out):
         offsets = keep.tile([P, S // GROUP], U16, name="offsets")
 
         word_rows = x_words[0].rearrange("p n r -> p (n r)").bitcast(I32)
-        word_table = keep.tile([P, T], I32, name="word_table", align_bytes=64)
+        word_table = keep.tile([P, T], I32, name="word_table", align_bytes=BURST)
         nc.sync.dma_start(word_table[:, :WORDS_AHEAD], word_rows[:, :WORDS_AHEAD])
         nc.sync.dma_start(offsets[:], offs)
 
-        scale_table = keep.tile([P, T], U8, name="scale_table", align_bytes=64)
+        scale_table = keep.tile([P, T], U8, name="scale_table", align_bytes=BURST)
         nc.vector.memset(scale_table[:].bitcast(I32), 0)
         for q in range(4):
             nc.sync.dma_start(scale_table[q:P:32, :].bitcast(I32), x_scales[0, q:SCALE_ROWS:4, :].bitcast(I32))
 
         nc.sync.dma_start(word_table[:, WORDS_AHEAD:], word_rows[:, WORDS_AHEAD:])
         h_rows = hT.rearrange("(p j) c -> p j c", j=PACK)
-        h_raw = [keep.tile([P, PACK, P], F32, name="h_raw%d" % a, align_bytes=64) for a in range(TILES)]
+        h_raw = [keep.tile([P, PACK, P], F32, name="h_raw%d" % a, align_bytes=BURST) for a in range(TILES)]
         for a in range(TILES):
             nc.sync.dma_start(h_raw[a][:], h_rows[:, :, a * P : (a + 1) * P])
 
@@ -75,7 +76,7 @@ def tile_picked_zlate_sig_p_kernel(tc, x_words, x_scales, hT, offs, out):
         first_code = keep.tile([P, FIRST], U32, name="first_code", align_bytes=64)
         gather_words(first_code[:], 0, FIRST)
         quantize_tile(0)
-        rest_code = keep.tile([P, S - FIRST], U32, name="rest_code", tag="h_raw0", align_bytes=64)
+        rest_code = keep.tile([P, S - FIRST], U32, name="rest_code", tag="h_raw0", align_bytes=BURST)
         for j0, j1 in ((FIRST, SECOND), (SECOND, S)):
             gather_words(rest_code[:, j0 - FIRST : j1 - FIRST], j0, j1)
         quantize_tile(1)
@@ -102,11 +103,11 @@ def tile_picked_zlate_sig_p_kernel(tc, x_words, x_scales, hT, offs, out):
         low = ((0, N),)
         high = ((N, FIRST), (FIRST, SECOND), (SECOND, S))
         half = G // 2
-        result = [keep.tile([P, G], F32, name="result%d" % a) for a in range(TILES)]
+        result = [keep.tile([P, G], F32, name="result%d" % a, align_bytes=BURST) for a in range(TILES)]
 
         def reduce_banks(a, banks, tag):
             c0, c1 = banks[0][0][0][0] // D, banks[-1][0][-1][1] // D
-            best = keep.tile([P, c1 - c0], F32, name="best%d_%d" % (a, c0), tag=tag, align_bytes=64)
+            best = keep.tile([P, c1 - c0], F32, name="best%d_%d" % (a, c0), tag=tag, align_bytes=BURST)
             for spans, bank in banks:
                 nc.vector.tensor_reduce(best[:, spans[0][0] // D - c0 : spans[-1][1] // D - c0], by_doc(scores(a, spans, bank)), AXIS_X, MAX)
             nc.scalar.activation(result[a][:, c0:c1], best[:], SIGMOID)

@@ -14,6 +14,9 @@ U8 = mybir.dt.uint8
 FP8X4 = mybir.dt.float8_e4m3fn_x4
 SIGMOID = mybir.ActivationFunctionType.Sigmoid
 MAX = mybir.AluOpType.max
+MIN = mybir.AluOpType.min
+ADD = mybir.AluOpType.add
+SUBTRACT = mybir.AluOpType.subtract
 AXIS_X = mybir.AxisListType.X
 
 P = 128
@@ -24,14 +27,15 @@ GROUP = 16
 SCALE_ROWS = K // 32
 BURST = 256
 WORDS_AHEAD = 384
-FIRST = 640
 SECOND = 768
+THIRD = 896
 
 
 def tile_picked_zlate_sig_p_kernel(tc, x_words, x_scales, hT, offs, out):
     nc = tc.nc
     with ExitStack() as ctx:
         keep = ctx.enter_context(tc.tile_pool(name="keep", bufs=1))
+        over = ctx.enter_context(tc.tile_pool(name="over", bufs=1))
         psum = ctx.enter_context(tc.psum_pool(name="psum", bufs=1))
 
         offsets = keep.tile([P, S // GROUP], U16, name="offsets")
@@ -46,20 +50,30 @@ def tile_picked_zlate_sig_p_kernel(tc, x_words, x_scales, hT, offs, out):
         for q in range(4):
             nc.sync.dma_start(scale_table[q:P:32, :].bitcast(I32), x_scales[0, q:SCALE_ROWS:4, :].bitcast(I32))
 
+        warm = keep.tile([P, 2], F32, name="warm")
+        nc.gpsimd.memset(warm[:, 0:1], 0.0)
+        nc.scalar.activation(warm[:, 1:2], warm[:, 0:1], SIGMOID)
+
         nc.sync.dma_start(word_table[:, WORDS_AHEAD:], word_rows[:, WORDS_AHEAD:])
         h_rows = hT.rearrange("(p j) c -> p j c", j=PACK)
-        h_raw = [keep.tile([P, PACK, P], F32, name="h_raw%d" % a, align_bytes=BURST) for a in range(TILES)]
-        for a in range(TILES):
-            nc.sync.dma_start(h_raw[a][:], h_rows[:, :, a * P : (a + 1) * P])
+        parts = [(0, 0, 2), (0, 2, PACK)] + [(a, 0, PACK) for a in range(1, TILES)]
+        place = {1: 8192, 2: 0, 3: 4096}
+        h_raw = []
+        for a, r0, r1 in parts:
+            if a in place:
+                h_raw.append(over.tile([P, PACK, P], F32, name="h_raw%d" % a, align_bytes=BURST, offset=place[a]))
+            else:
+                h_raw.append(keep.tile([P, r1 - r0, P], F32, name="h_raw_%d_%d" % (a, r0), tag="h_raw%d" % a if r1 == PACK else "h_head", align_bytes=BURST))
+            nc.sync.dma_start(h_raw[-1][:], h_rows[:, r0:r1, a * P : (a + 1) * P])
 
         x_scale = keep.tile([P, S], U8, name="x_scale", align_bytes=64)
         nc.vector.tensor_copy(x_scale[:], scale_table[:].indirect(offsets[:]))
 
         grouped = [keep.tile([P, P, PACK], BF16, name="grouped%d" % a, align_bytes=64) for a in range(TILES)]
-        for a in range(TILES):
+        for raw, (a, r0, r1) in zip(h_raw, parts):
             nc.scalar.copy(
-                grouped[a][:].rearrange("p (c i) j -> p c j i", i=4),
-                h_raw[a][:].rearrange("p j (c i) -> p c j i", i=4),
+                grouped[a][:, :, r0:r1].rearrange("p (c i) j -> p c j i", i=4),
+                raw[:].rearrange("p j (c i) -> p c j i", i=4),
             )
 
         h_code = {}
@@ -73,24 +87,32 @@ def tile_picked_zlate_sig_p_kernel(tc, x_words, x_scales, hT, offs, out):
         def gather_words(picked, j0, j1):
             nc.vector.tensor_copy(picked, word_table[:].bitcast(U32).indirect(offsets[:, j0 // GROUP : j1 // GROUP]))
 
-        first_code = keep.tile([P, FIRST], U32, name="first_code", align_bytes=64)
-        gather_words(first_code[:], 0, FIRST)
+        first_code = keep.tile([P, N], U32, name="first_code", align_bytes=64)
+        gather_words(first_code[:], 0, N)
         quantize_tile(0)
-        rest_code = keep.tile([P, S - FIRST], U32, name="rest_code", tag="h_raw0", align_bytes=BURST)
-        for j0, j1 in ((FIRST, SECOND), (SECOND, S)):
-            gather_words(rest_code[:, j0 - FIRST : j1 - FIRST], j0, j1)
+        second_code = keep.tile([P, THIRD - N], U32, name="second_code", tag="h_raw0", align_bytes=BURST)
+        for j0, j1 in ((N, SECOND), (SECOND, THIRD)):
+            gather_words(second_code[:, j0 - N : j1 - N], j0, j1)
         quantize_tile(1)
+        third_code = over.tile([P, S - THIRD], U32, name="third_code", align_bytes=BURST, offset=8192)
+        gather_words(third_code[:], THIRD, S)
+
+        def codes(j0, j1):
+            if j1 <= N:
+                return first_code[:, j0:j1]
+            if j1 <= THIRD:
+                return second_code[:, j0 - N : j1 - N]
+            return third_code[:]
 
         def scores(a, spans, tag):
             base = spans[0][0]
             bank = psum.tile([P, N], F32, name="bank%d_%d" % (a, base), tag=tag)
             for j0, j1 in spans:
-                codes = first_code[:, j0:j1] if j1 <= FIRST else rest_code[:, j0 - FIRST : j1 - FIRST]
                 nc.tensor.matmul_mx(
                     out=bank[:, j0 - base : j1 - base],
                     lhsT=h_code[a][:].bitcast(FP8X4),
                     lhsT_scale=h_scale[a][:],
-                    rhs=codes.bitcast(FP8X4),
+                    rhs=codes(j0, j1).bitcast(FP8X4),
                     rhs_scale=x_scale[:, j0:j1],
                     start=True,
                     stop=True,
@@ -101,34 +123,58 @@ def tile_picked_zlate_sig_p_kernel(tc, x_words, x_scales, hT, offs, out):
             return t.rearrange("p (v d) -> p v d", d=D)
 
         low = ((0, N),)
-        high = ((N, FIRST), (FIRST, SECOND), (SECOND, S))
+        high = ((N, SECOND), (SECOND, THIRD), (THIRD, S))
         half = G // 2
-        result = [keep.tile([P, G], F32, name="result%d" % a, align_bytes=BURST) for a in range(TILES)]
+        result0 = over.tile([P, G], F32, name="result0", align_bytes=BURST, offset=4352)
+        results12 = over.tile([P, 2, G], F32, name="results12", align_bytes=BURST, offset=5632)
+        result3 = keep.tile([P, G], F32, name="result3", align_bytes=BURST)
+        result = [result0[:], results12[:, 0, :], results12[:, 1, :], result3[:]]
 
-        def reduce_banks(a, banks, tag):
-            c0, c1 = banks[0][0][0][0] // D, banks[-1][0][-1][1] // D
-            best = keep.tile([P, c1 - c0], F32, name="best%d_%d" % (a, c0), tag=tag, align_bytes=BURST)
-            for spans, bank in banks:
-                nc.vector.tensor_reduce(best[:, spans[0][0] // D - c0 : spans[-1][1] // D - c0], by_doc(scores(a, spans, bank)), AXIS_X, MAX)
-            nc.scalar.activation(result[a][:, c0:c1], best[:], SIGMOID)
+        waiting = []
+
+        def reduce_bank(a, spans, bank, offset=None):
+            c0, c1 = spans[0][0] // D, spans[-1][1] // D
+            if offset is None:
+                best = keep.tile([P, c1 - c0], F32, name="best%d_%d" % (a, c0))
+            else:
+                best = over.tile([P, c1 - c0], F32, name="best%d_%d" % (a, c0), align_bytes=BURST, offset=offset)
+            nc.vector.tensor_reduce(best[:], by_doc(scores(a, spans, bank)), AXIS_X, MAX)
+            waiting.append((result[a][:, c0:c1], best))
+
+        def squash_waiting():
+            for target, best in waiting:
+                nc.scalar.activation(target, best[:], SIGMOID)
+            waiting.clear()
 
         def store(a, c0, c1):
             nc.sync.dma_start(out[a * P : (a + 1) * P, c0:c1], result[a][:, c0:c1])
 
-        reduce_banks(0, ((low, "b0"),), "best0")
-        reduce_banks(0, ((high[:2], "b1"),), "best1")
+        reduce_bank(0, low, "b0", 8704)
         quantize_tile(2)
-        reduce_banks(0, ((high[2:], "b2"),), "h_raw2")
-        store(0, 0, G)
+        reduce_bank(1, low, "b1", 0)
+        early = over.tile([P, N], F32, name="early", align_bytes=BURST, offset=2304)
+        nc.scalar.activation(early[:], scores(0, high, "b2"), SIGMOID)
+        sides = early[:].rearrange("p (v r i) -> p r v i", r=2, i=D // 2)
+        gap = keep.tile([P, half, D // 2], F32, name="gap")
+        nc.gpsimd.tensor_tensor(gap[:], sides[:, 0], sides[:, 1], SUBTRACT)
+        excess = keep.tile([P, half, D // 2], F32, name="excess")
+        nc.gpsimd.tensor_scalar(excess[:], gap[:], 1.0, 0.0, MIN, MAX)
+        larger = keep.tile([P, half, D // 2], F32, name="larger")
+        nc.gpsimd.tensor_tensor(larger[:], excess[:], sides[:, 1], ADD)
+
         quantize_tile(3)
-        reduce_banks(1, ((low, "b3"), (high, "b4")), "h_raw3")
-        store(1, 0, G)
-        reduce_banks(2, ((low, "b5"),), "best2")
+        reduce_bank(1, high, "b3", 4864)
+        squash_waiting()
+        store(0, 0, half)
+        reduce_bank(2, low, "b4", 5120)
+        reduce_bank(2, high, "b5", 5376)
         squashed = keep.tile([P, N], F32, name="squashed")
-        reduce_banks(2, ((high, "b6"),), "best3")
-        store(2, 0, G)
-        nc.scalar.activation(squashed[:], scores(3, high, "b7"), SIGMOID)
-        reduce_banks(3, ((low, "b0"),), "best4")
-        store(3, 0, half)
+        nc.scalar.activation(squashed[:], scores(3, high, "b6"), SIGMOID)
+        squash_waiting()
+        nc.sync.dma_start(out[P : 3 * P, :].rearrange("(a p) v -> p a v", p=P), results12[:])
+        reduce_bank(3, low, "b7")
         nc.vector.tensor_reduce(result[3][:, half:], by_doc(squashed[:]), AXIS_X, MAX)
-        store(3, half, G)
+        squash_waiting()
+        store(3, 0, G)
+        nc.vector.tensor_reduce(result[0][:, half:], larger[:], AXIS_X, MAX)
+        store(0, half, G)

@@ -28,7 +28,7 @@ SCALE_ROWS = K // 32
 BURST = 256
 WORDS_AHEAD = 384
 SECOND = 768
-THIRD = 896
+HALVED = 56
 
 
 def tile_picked_zlate_sig_p_kernel(tc, x_words, x_scales, hT, offs, out):
@@ -56,14 +56,14 @@ def tile_picked_zlate_sig_p_kernel(tc, x_words, x_scales, hT, offs, out):
 
         nc.sync.dma_start(word_table[:, WORDS_AHEAD:], word_rows[:, WORDS_AHEAD:])
         h_rows = hT.rearrange("(p j) c -> p j c", j=PACK)
-        parts = [(0, 0, 2), (0, 2, PACK)] + [(a, 0, PACK) for a in range(1, TILES)]
+        parts = [(0, 0, 2), (0, 2, PACK), (1, 0, 2), (1, 2, PACK)] + [(a, 0, PACK) for a in range(2, TILES)]
         place = {1: 8192, 2: 0, 3: 4096}
         h_raw = []
         for a, r0, r1 in parts:
-            if a in place:
-                h_raw.append(over.tile([P, PACK, P], F32, name="h_raw%d" % a, align_bytes=BURST, offset=place[a]))
+            if a in place and r1 == PACK:
+                h_raw.append(over.tile([P, r1 - r0, P], F32, name="h_raw%d" % a, align_bytes=BURST, offset=place[a]))
             else:
-                h_raw.append(keep.tile([P, r1 - r0, P], F32, name="h_raw_%d_%d" % (a, r0), tag="h_raw%d" % a if r1 == PACK else "h_head", align_bytes=BURST))
+                h_raw.append(keep.tile([P, r1 - r0, P], F32, name="h_raw_%d_%d" % (a, r0), tag="h_raw%d" % a if r1 == PACK else "h_head%d" % a, align_bytes=BURST))
             nc.sync.dma_start(h_raw[-1][:], h_rows[:, r0:r1, a * P : (a + 1) * P])
 
         x_scale = keep.tile([P, S], U8, name="x_scale", align_bytes=64)
@@ -90,18 +90,17 @@ def tile_picked_zlate_sig_p_kernel(tc, x_words, x_scales, hT, offs, out):
         first_code = keep.tile([P, N], U32, name="first_code", align_bytes=64)
         gather_words(first_code[:], 0, N)
         quantize_tile(0)
-        second_code = keep.tile([P, THIRD - N], U32, name="second_code", tag="h_raw0", align_bytes=BURST)
-        for j0, j1 in ((N, SECOND), (SECOND, THIRD)):
-            gather_words(second_code[:, j0 - N : j1 - N], j0, j1)
+        second_code = keep.tile([P, SECOND - N], U32, name="second_code", tag="h_raw0", align_bytes=BURST)
+        gather_words(second_code[:], N, SECOND)
         quantize_tile(1)
-        third_code = over.tile([P, S - THIRD], U32, name="third_code", align_bytes=BURST, offset=8192)
-        gather_words(third_code[:], THIRD, S)
+        third_code = over.tile([P, S - SECOND], U32, name="third_code", align_bytes=BURST, offset=8192 - 768)
+        gather_words(third_code[:], SECOND, S)
 
         def codes(j0, j1):
             if j1 <= N:
                 return first_code[:, j0:j1]
-            if j1 <= THIRD:
-                return second_code[:, j0 - N : j1 - N]
+            if j1 <= SECOND:
+                return second_code[:]
             return third_code[:]
 
         def scores(a, spans, tag):
@@ -123,7 +122,7 @@ def tile_picked_zlate_sig_p_kernel(tc, x_words, x_scales, hT, offs, out):
             return t.rearrange("p (v d) -> p v d", d=D)
 
         low = ((0, N),)
-        high = ((N, SECOND), (SECOND, THIRD), (THIRD, S))
+        high = ((N, SECOND), (SECOND, S))
         half = G // 2
         result0 = over.tile([P, G], F32, name="result0", align_bytes=BURST, offset=4352)
         results12 = over.tile([P, 2, G], F32, name="results12", align_bytes=BURST, offset=5632)
@@ -153,28 +152,30 @@ def tile_picked_zlate_sig_p_kernel(tc, x_words, x_scales, hT, offs, out):
         quantize_tile(2)
         reduce_bank(1, low, "b1", 0)
         early = over.tile([P, N], F32, name="early", align_bytes=BURST, offset=2304)
-        nc.scalar.activation(early[:], scores(0, high, "b2"), SIGMOID)
-        sides = early[:].rearrange("p (v r i) -> p r v i", r=2, i=D // 2)
-        gap = keep.tile([P, half, D // 2], F32, name="gap")
+        bank = scores(0, high, "b2")
+        for c0, c1 in ((0, HALVED * D), (HALVED * D, N)):
+            nc.scalar.activation(early[:, c0:c1], bank[:, c0:c1], SIGMOID)
+        sides = early[:, : HALVED * D].rearrange("p (v r i) -> p r v i", r=2, i=D // 2)
+        gap = keep.tile([P, HALVED, D // 2], F32, name="gap")
         nc.gpsimd.tensor_tensor(gap[:], sides[:, 0], sides[:, 1], SUBTRACT)
-        excess = keep.tile([P, half, D // 2], F32, name="excess")
+        excess = keep.tile([P, HALVED, D // 2], F32, name="excess")
         nc.gpsimd.tensor_scalar(excess[:], gap[:], 1.0, 0.0, MIN, MAX)
-        larger = keep.tile([P, half, D // 2], F32, name="larger")
+        larger = keep.tile([P, HALVED, D // 2], F32, name="larger")
         nc.gpsimd.tensor_tensor(larger[:], excess[:], sides[:, 1], ADD)
 
         quantize_tile(3)
         reduce_bank(1, high, "b3", 4864)
         squash_waiting()
-        store(0, 0, half)
         reduce_bank(2, low, "b4", 5120)
         reduce_bank(2, high, "b5", 5376)
         squashed = keep.tile([P, N], F32, name="squashed")
         nc.scalar.activation(squashed[:], scores(3, high, "b6"), SIGMOID)
         squash_waiting()
         nc.sync.dma_start(out[P : 3 * P, :].rearrange("(a p) v -> p a v", p=P), results12[:])
+        nc.vector.tensor_reduce(result[0][:, half + HALVED :], by_doc(early[:, HALVED * D :]), AXIS_X, MAX)
         reduce_bank(3, low, "b7")
         nc.vector.tensor_reduce(result[3][:, half:], by_doc(squashed[:]), AXIS_X, MAX)
         squash_waiting()
         store(3, 0, G)
-        nc.vector.tensor_reduce(result[0][:, half:], larger[:], AXIS_X, MAX)
-        store(0, half, G)
+        nc.vector.tensor_reduce(result[0][:, half : half + HALVED], larger[:], AXIS_X, MAX)
+        store(0, 0, G)

from contextlib import ExitStack

import concourse.mybir as mybir

K, T, S, D, G, J = 512, 2048, 1024, 8, 128, 512
FLOPS = 2 * K * J * S

F32 = mybir.dt.float32
BF16 = mybir.dt.bfloat16
I32 = mybir.dt.int32
U32 = mybir.dt.uint32
U16 = mybir.dt.uint16
U8 = mybir.dt.uint8
FP8X4 = mybir.dt.float8_e4m3fn_x4
SIGMOID = mybir.ActivationFunctionType.Sigmoid
MAX = mybir.AluOpType.max
MIN = mybir.AluOpType.min
ADD = mybir.AluOpType.add
SUBTRACT = mybir.AluOpType.subtract
AXIS_X = mybir.AxisListType.X

P = 128
PACK = 4
N = 512
TILES = J // P
GROUP = 16
SCALE_ROWS = K // 32
BURST = 256
WORDS_AHEAD = 384
SECOND = 768
HALVED = 56


def tile_picked_zlate_sig_p_kernel(tc, x_words, x_scales, hT, offs, out):
    nc = tc.nc
    with ExitStack() as ctx:
        keep = ctx.enter_context(tc.tile_pool(name="keep", bufs=1))
        over = ctx.enter_context(tc.tile_pool(name="over", bufs=1))
        psum = ctx.enter_context(tc.psum_pool(name="psum", bufs=1))

        offsets = keep.tile([P, S // GROUP], U16, name="offsets")

        word_rows = x_words[0].rearrange("p n r -> p (n r)").bitcast(I32)
        word_table = keep.tile([P, T], I32, name="word_table", align_bytes=BURST)
        nc.sync.dma_start(word_table[:, :WORDS_AHEAD], word_rows[:, :WORDS_AHEAD])
        nc.sync.dma_start(offsets[:], offs)

        scale_table = keep.tile([P, T], U8, name="scale_table", align_bytes=BURST)
        nc.vector.memset(scale_table[:].bitcast(I32), 0)
        for q in range(4):
            nc.sync.dma_start(scale_table[q:P:32, :].bitcast(I32), x_scales[0, q:SCALE_ROWS:4, :].bitcast(I32))

        warm = keep.tile([P, 2], F32, name="warm")
        nc.gpsimd.memset(warm[:, 0:1], 0.0)
        nc.scalar.activation(warm[:, 1:2], warm[:, 0:1], SIGMOID)

        nc.sync.dma_start(word_table[:, WORDS_AHEAD:], word_rows[:, WORDS_AHEAD:])
        h_rows = hT.rearrange("(p j) c -> p j c", j=PACK)
        parts = [(0, 0, 2), (0, 2, PACK), (1, 0, 2), (1, 2, PACK)] + [(a, 0, PACK) for a in range(2, TILES)]
        place = {1: 8192, 2: 0, 3: 4096}
        h_raw = []
        for a, r0, r1 in parts:
            if a in place and r1 == PACK:
                h_raw.append(over.tile([P, r1 - r0, P], F32, name="h_raw%d" % a, align_bytes=BURST, offset=place[a]))
            else:
                h_raw.append(keep.tile([P, r1 - r0, P], F32, name="h_raw_%d_%d" % (a, r0), tag="h_raw%d" % a if r1 == PACK else "h_head%d" % a, align_bytes=BURST))
            nc.sync.dma_start(h_raw[-1][:], h_rows[:, r0:r1, a * P : (a + 1) * P])

        x_scale = keep.tile([P, S], U8, name="x_scale", align_bytes=64)
        nc.vector.tensor_copy(x_scale[:], scale_table[:].indirect(offsets[:]))

        grouped = [keep.tile([P, P, PACK], BF16, name="grouped%d" % a, align_bytes=64) for a in range(TILES)]
        for raw, (a, r0, r1) in zip(h_raw, parts):
            nc.scalar.copy(
                grouped[a][:, :, r0:r1].rearrange("p (c i) j -> p c j i", i=4),
                raw[:].rearrange("p j (c i) -> p c j i", i=4),
            )

        h_code = {}
        h_scale = {}

        def quantize_tile(a):
            h_code[a] = keep.tile([P, P], U32, name="h_code%d" % a, align_bytes=64)
            h_scale[a] = keep.tile([P, P], U8, name="h_scale%d" % a, align_bytes=64)
            nc.vector.quantize_mx(out=h_code[a][:].bitcast(FP8X4), scales=h_scale[a][:], in_=grouped[a][:].rearrange("p c j -> p (c j)"))

        def gather_words(picked, j0, j1):
            nc.vector.tensor_copy(picked, word_table[:].bitcast(U32).indirect(offsets[:, j0 // GROUP : j1 // GROUP]))

        first_code = keep.tile([P, N], U32, name="first_code", align_bytes=64)
        gather_words(first_code[:], 0, N)
        quantize_tile(0)
        second_code = keep.tile([P, SECOND - N], U32, name="second_code", tag="h_raw0", align_bytes=BURST)
        gather_words(second_code[:], N, SECOND)
        quantize_tile(1)
        third_code = over.tile([P, S - SECOND], U32, name="third_code", align_bytes=BURST, offset=8192 - 768)
        gather_words(third_code[:], SECOND, S)

        def codes(j0, j1):
            if j1 <= N:
                return first_code[:, j0:j1]
            if j1 <= SECOND:
                return second_code[:]
            return third_code[:]

        def scores(a, spans, tag):
            base = spans[0][0]
            bank = psum.tile([P, N], F32, name="bank%d_%d" % (a, base), tag=tag)
            for j0, j1 in spans:
                nc.tensor.matmul_mx(
                    out=bank[:, j0 - base : j1 - base],
                    lhsT=h_code[a][:].bitcast(FP8X4),
                    lhsT_scale=h_scale[a][:],
                    rhs=codes(j0, j1).bitcast(FP8X4),
                    rhs_scale=x_scale[:, j0:j1],
                    start=True,
                    stop=True,
                )
            return bank[:, : spans[-1][1] - base]

        def by_doc(t):
            return t.rearrange("p (v d) -> p v d", d=D)

        low = ((0, N),)
        high = ((N, SECOND), (SECOND, S))
        half = G // 2
        result0 = over.tile([P, G], F32, name="result0", align_bytes=BURST, offset=4352)
        results12 = over.tile([P, 2, G], F32, name="results12", align_bytes=BURST, offset=5632)
        result3 = keep.tile([P, G], F32, name="result3", align_bytes=BURST)
        result = [result0[:], results12[:, 0, :], results12[:, 1, :], result3[:]]

        waiting = []

        def reduce_bank(a, spans, bank, offset=None):
            c0, c1 = spans[0][0] // D, spans[-1][1] // D
            if offset is None:
                best = keep.tile([P, c1 - c0], F32, name="best%d_%d" % (a, c0))
            else:
                best = over.tile([P, c1 - c0], F32, name="best%d_%d" % (a, c0), align_bytes=BURST, offset=offset)
            nc.vector.tensor_reduce(best[:], by_doc(scores(a, spans, bank)), AXIS_X, MAX)
            waiting.append((result[a][:, c0:c1], best))

        def squash_waiting():
            for target, best in waiting:
                nc.scalar.activation(target, best[:], SIGMOID)
            waiting.clear()

        def store(a, c0, c1):
            nc.sync.dma_start(out[a * P : (a + 1) * P, c0:c1], result[a][:, c0:c1])

        reduce_bank(0, low, "b0", 8704)
        quantize_tile(2)
        reduce_bank(1, low, "b1", 0)
        early = over.tile([P, N], F32, name="early", align_bytes=BURST, offset=2304)
        bank = scores(0, high, "b2")
        for c0, c1 in ((0, HALVED * D), (HALVED * D, N)):
            nc.scalar.activation(early[:, c0:c1], bank[:, c0:c1], SIGMOID)
        sides = early[:, : HALVED * D].rearrange("p (v r i) -> p r v i", r=2, i=D // 2)
        gap = keep.tile([P, HALVED, D // 2], F32, name="gap")
        nc.gpsimd.tensor_tensor(gap[:], sides[:, 0], sides[:, 1], SUBTRACT)
        excess = keep.tile([P, HALVED, D // 2], F32, name="excess")
        nc.gpsimd.tensor_scalar(excess[:], gap[:], 1.0, 0.0, MIN, MAX)
        larger = keep.tile([P, HALVED, D // 2], F32, name="larger")
        nc.gpsimd.tensor_tensor(larger[:], excess[:], sides[:, 1], ADD)

        quantize_tile(3)
        reduce_bank(1, high, "b3", 4864)
        squash_waiting()
        reduce_bank(2, low, "b4", 5120)
        reduce_bank(2, high, "b5", 5376)
        squashed = keep.tile([P, N], F32, name="squashed")
        nc.scalar.activation(squashed[:], scores(3, high, "b6"), SIGMOID)
        squash_waiting()
        nc.sync.dma_start(out[P : 3 * P, :].rearrange("(a p) v -> p a v", p=P), results12[:])
        nc.vector.tensor_reduce(result[0][:, half + HALVED :], by_doc(early[:, HALVED * D :]), AXIS_X, MAX)
        reduce_bank(3, low, "b7")
        nc.vector.tensor_reduce(result[3][:, half:], by_doc(squashed[:]), AXIS_X, MAX)
        squash_waiting()
        store(3, 0, G)
        nc.vector.tensor_reduce(result[0][:, half : half + HALVED], larger[:], AXIS_X, MAX)
        store(0, 0, G)
